import numpy as np
import ml_dtypes


def mxq(x, axis, fmt="e4m3"):
    dtype, down = {"e4m3": (ml_dtypes.float8_e4m3fn, 7), "e5m2": (ml_dtypes.float8_e5m2, 14)}[fmt]
    v = np.moveaxis(np.asarray(x, np.float32).astype(ml_dtypes.bfloat16).astype(np.float64), axis, -1)
    blocks = v.reshape(v.shape[:-1] + (-1, 32))
    amax = np.abs(blocks).max(-1, keepdims=True)
    byte = np.maximum(np.where(amax > 0, np.frexp(amax)[1] - 1 + 127, 0) - down, 1)
    scale = np.exp2(byte - 127.0)
    codes = (blocks / scale).astype(np.float32).astype(dtype).astype(np.float64)
    return np.moveaxis((codes * scale).reshape(v.shape), -1, axis)


WIDE = False


def mx_kscale(k):
    if not WIDE:
        return np.ones(k)
    levels = np.array([10, -10, 5, -5, 0])
    if k % 512:
        return np.exp2(np.random.permutation(np.resize(levels, k // 32))).repeat(32)
    a = np.empty((k // 512, 16))
    for p in range(k // 512):
        a[p, :8] = np.random.permutation(np.resize(levels, 8))
        for g in range(8):
            far = levels[np.abs(levels - a[p, g]) >= 10]
            a[p, g + 8] = far[np.random.randint(len(far))]
    return np.exp2(a.ravel()).repeat(32)


def f64(x):
    return np.asarray(x).astype(np.float64)


def striped(idx):
    return np.tile(idx.reshape(-1, 16).T, (8, 1)).astype(np.uint16)


def unstriped(offs):
    return offs[:16].T.reshape(-1).astype(np.int64)


E2M1 = np.array([0.0, 0.5, 1.0, 1.5, 2.0, 3.0, 4.0, 6.0, -0.0, -0.5, -1.0, -1.5, -2.0, -3.0, -4.0, -6.0])


def pack_weight(w, fmt):
    k, n = w.shape
    w = f64(np.asarray(w, np.float32).astype(ml_dtypes.bfloat16)).reshape(k // 32, 32, n)
    amax = np.abs(w).max(1)
    if fmt == "e4m3":
        byte = np.frexp(amax)[1] - 1 + 127 - 7
    else:
        mant, ex = np.frexp(amax / 6.0)
        byte = np.where(mant > 0.5, ex, ex - 1) + 127
    byte = np.clip(np.where(amax > 0, byte, 1), 1, 254)
    scaled = (w * np.exp2(127.0 - byte)[:, None, :]).reshape(k, n).astype(np.float32)
    by_word = np.ascontiguousarray(scaled.reshape(k // 512, 128, 4, n).transpose(0, 1, 3, 2))
    if fmt == "e4m3":
        words = by_word.astype(ml_dtypes.float8_e4m3fn).view(np.uint8)
    else:
        c = by_word.astype(ml_dtypes.float4_e2m1fn).view(np.uint8) & 0xF
        words = (c[..., 0::2] | (c[..., 1::2] << 4)).reshape(k // 512, 128, 2 * n)
    return np.ascontiguousarray(words), np.ascontiguousarray(byte.astype(np.uint8).reshape(k // 512, 16, n))


def unpack_weight(words, scales, fmt):
    g, _, n = scales.shape
    words = np.ascontiguousarray(words).reshape(g, 128, n, -1)
    if fmt == "e4m3":
        vals = words.view(ml_dtypes.float8_e4m3fn).astype(np.float64)
    else:
        nib = np.empty((g, 128, n, 4), np.uint8)
        nib[..., 0::2] = words & 0xF
        nib[..., 1::2] = words >> 4
        vals = E2M1[nib]
    vals = vals * np.repeat(np.exp2(scales.astype(np.float64) - 127.0), 8, axis=1)[..., None]
    return vals.transpose(0, 1, 3, 2).reshape(g * 512, n)


def gelu(v):
    return 0.5 * v * (1.0 + np.tanh(np.sqrt(2.0 / np.pi) * (v + 0.044715 * v**3)))


K, H, N, T, S, P = 1024, 1024, 512, 4096, 1024, 512

def setup_inputs():
    n = np.random.standard_normal
    s = mx_kscale(K)[:, None]
    u = mx_kscale(H)[:, None]
    tab_words, tab_scales = pack_weight(n((K, T)) * s, "e4m3")
    wa_words, wa_scales = pack_weight(n((H, N)) / np.sqrt(H) / u, "e2m1")
    return {
        "tab_words": tab_words, "tab_scales": tab_scales,
        "offs": striped(np.random.permutation(T)[:S]),
        "pos1": striped(np.random.permutation(S)[:P]),
        "pos2": striped(np.random.permutation(S)[:P]),
        "w1": (1.5 * n((K, H)) / np.sqrt(K) / s).astype(np.float32),
        "gain": (np.exp(0.3 * n(H)) * u[:, 0]).astype(np.float32),
        "visit": (0.6 * n((H, S)) * u).astype(np.float32),
        "pain": np.exp(0.5 * n(H)).astype(np.float32),
        "breath": (0.5 * n(H) * u[:, 0]).astype(np.float32),
        "wa_words": wa_words, "wa_scales": wa_scales,
        "wb": (1.2 * n((H, N)) / np.sqrt(H) / u).astype(np.float32),
    }

def reference(tab_words, tab_scales, offs, pos1, pos2, w1, gain, visit, pain, breath, wa_words, wa_scales, wb):
    v = unpack_weight(tab_words, tab_scales, "e4m3")[:, unstriped(offs)]
    e = mxq(f64(w1), 0, "e4m3").T @ v
    h = f64(gain)[:, None] * np.tanh(e) + f64(visit)
    xa = h[:, unstriped(pos1)] * f64(pain)[:, None]
    xb = np.maximum(h[:, unstriped(pos2)], f64(breath)[:, None])
    wa = unpack_weight(wa_words, wa_scales, "e2m1")
    ya = wa.T @ mxq(xa, 0, "e4m3")
    yb = mxq(f64(wb), 0, "e4m3").T @ mxq(xb, 0, "e4m3")
    return np.maximum(ya, yb) + ya

@@ -1,0 +1,323 @@
+from contextlib import ExitStack
+
+import concourse.mybir as mybir
+
+K, H, N, T, S, PICKS = 1024, 1024, 512, 4096, 1024, 512
+FLOPS = 2 * K * H * S + 2 * 2 * H * N * PICKS
+
+F32 = mybir.dt.float32
+BF16 = mybir.dt.bfloat16
+I32 = mybir.dt.int32
+U32 = mybir.dt.uint32
+U16 = mybir.dt.uint16
+U8 = mybir.dt.uint8
+FP8X4 = mybir.dt.float8_e4m3fn_x4
+FP4X4 = mybir.dt.float4_e2m1fn_x4
+ALU = mybir.AluOpType
+ACT = mybir.ActivationFunctionType
+
+P = 128
+PACK = 4
+K_PASS = P * PACK
+PASSES = 2
+BANK = 512
+BANKS = 8
+LIST = 16
+HALF = PICKS // 2
+ROW_TILES = PASSES * PACK
+
+
+def tile_list_symptom_diary_features_kernel(
+    tc, tab_words, tab_scales, offs, pos1, pos2, w1, gain, visit, pain, breath, wa_words, wa_scales, wb, out
+):
+    nc = tc.nc
+    with ExitStack() as ctx:
+        lists = ctx.enter_context(tc.tile_pool(name="lists", bufs=1))
+        keep = ctx.enter_context(tc.tile_pool(name="keep", bufs=1))
+        ring = ctx.enter_context(tc.tile_pool(name="ring", bufs=2))
+        psum = ctx.enter_context(tc.psum_pool(name="psum", bufs=1))
+
+        def bank(k, name):
+            return psum.tile([P, BANK], F32, name=name, tag="bank%d" % k)
+
+        def load_list(src, name):
+            tile = lists.tile([P, src.shape[1]], U16, name=name)
+            nc.sync.dma_start(tile[:], src)
+            return tile
+
+        def load_rows(src, name):
+            raw = ring.tile([P, PACK, BANK], F32, name=name, tag="raw", bufs=3)
+            nc.sync.dma_start(raw[:], src.rearrange("(p j) c -> p j c", j=PACK))
+            return raw
+
+        def load_table(a, pieces):
+            words = keep.tile([P, T], U32, name="tab_words%d" % a)
+            src = tab_words[a].rearrange("p t i -> p (t i)").bitcast(I32)
+            step = T // pieces
+            for c in range(0, T, step):
+                nc.sync.dma_start(words[:, c : c + step].bitcast(I32), src[:, c : c + step])
+            return words
+
+        def load_vector(src, name):
+            tile = keep.tile([P, PASSES, 2 * PACK], F32, name=name)
+            nc.sync.dma_start(tile[:, :, 0:PACK], src.rearrange("(b p t) -> p b t", b=PASSES, t=PACK))
+            return tile
+
+        def load_visit(i):
+            b, t = divmod(i, PACK)
+            tile = keep.tile([P, S], F32, name="visit%d" % i)
+            nc.sync.dma_start(tile[:], visit.rearrange("(b p t) j -> b t p j", b=PASSES, t=PACK)[b, t])
+            return tile
+
+        def w1_block(a, b):
+            return w1[a * K_PASS : (a + 1) * K_PASS, b * K_PASS : (b + 1) * K_PASS]
+
+        tab_plane = keep.tile([P, T], U8, name="tab_plane")
+        nc.vector.memset(tab_plane[:].bitcast(I32), 0)
+        wa_plane = keep.tile([P, PASSES, N], U8, name="wa_plane", align_bytes=64)
+        nc.vector.memset(wa_plane[:].rearrange("p a c -> p (a c)").bitcast(I32), 0)
+        tab_sb, w1_raw, wb_raw, visit_sb = {}, {}, {}, {}
+        offs_sb = load_list(offs, "offs_sb")
+        pos2_sb = load_list(pos2, "pos2_sb")
+        pos1_sb = load_list(pos1, "pos1_sb")
+        gain_sb = load_vector(gain, "gain_sb")
+        tab_sb[0] = load_table(0, 4)
+        for q in range(4):
+            nc.scalar.dma_start(
+                tab_plane[32 * q : 32 * q + 4 * PASSES, :].bitcast(I32), tab_scales[:, 4 * q : 4 * q + 4, :].bitcast(I32)
+            )
+        w1_raw[0, 0] = load_rows(w1_block(0, 0), "w1_raw")
+        tab_sb[1] = load_table(1, 1)
+        w1_last = []
+        for half in range(2):
+            raw = keep.tile([P, PACK, HALF], F32, name="w1_last%d" % half)
+            nc.sync.dma_start(
+                raw[:], w1_block(1, 0)[:, half * HALF : (half + 1) * HALF].rearrange("(p j) c -> p j c", j=PACK)
+            )
+            w1_last.append(raw)
+        visit_sb[0] = load_visit(0)
+        breath_sb = load_vector(breath, "breath_sb")
+        pain_sb = load_vector(pain, "pain_sb")
+        for a in range(PASSES):
+            visit_sb[1 + a] = load_visit(1 + a)
+            w1_raw[a, 1] = load_rows(w1_block(a, 1), "w1_raw")
+        for b in range(PASSES):
+            visit_sb[3 + b] = load_visit(3 + b)
+            wb_raw[b] = load_rows(wb[b * K_PASS : (b + 1) * K_PASS, :], "wb_raw")
+        for i in range(5, ROW_TILES):
+            visit_sb[i] = load_visit(i)
+        wa_sb = keep.tile([P, PASSES, 2 * N], U8, name="wa_sb", align_bytes=64)
+        nc.sync.dma_start(wa_sb[:].bitcast(I32), wa_words.rearrange("a p c -> p a c").bitcast(I32))
+        for q in range(4):
+            nc.sync.dma_start(
+                wa_plane[32 * q : 32 * q + 4].bitcast(I32),
+                wa_scales[:, 4 * q : 4 * q + 4, :].rearrange("a r c -> r a c").bitcast(I32),
+            )
+
+        def copy_on(engine, dst, src):
+            if engine == "scalar":
+                nc.scalar.copy(dst, src)
+            else:
+                nc.vector.tensor_copy(dst, src)
+
+        def woven_tile(width, tag="woven", bufs=3):
+            return ring.tile([P, PACK * width], BF16, name="woven", tag=tag, bufs=bufs, align_bytes=64)
+
+        def weave(engine, rows, width, tag="woven", bufs=3):
+            woven = woven_tile(width, tag, bufs)
+            copy_on(
+                engine,
+                woven[:].rearrange("p (c i j) -> p c j i", i=4, j=PACK),
+                rows[:].rearrange("p j (c i) -> p c j i", i=4),
+            )
+            return woven
+
+        def weave_w1(engine, raw):
+            woven = woven_tile(BANK)
+            copy_on(
+                engine,
+                woven[:].rearrange("p (t m j) -> p m j t", t=PACK, j=PACK),
+                raw[:].rearrange("p j (m t) -> p m j t", t=PACK),
+            )
+            return woven
+
+        def quantise(woven, width, name, pieces=1):
+            codes = keep.tile([P, width], U32, name=name + "_codes", align_bytes=64)
+            plane = keep.tile([P, width], U8, name=name + "_plane", align_bytes=64)
+            step = width // pieces
+            for c in range(0, width, step):
+                nc.vector.quantize_mx(
+                    out=codes[:, c : c + step].bitcast(FP8X4),
+                    scales=plane[:, c : c + step],
+                    in_=woven[:, PACK * c : PACK * (c + step)],
+                )
+            return codes, plane
+
+        v_words = [keep.tile([P, S], U32, name="v_words%d" % a, align_bytes=64) for a in range(PASSES)]
+        v_plane = keep.tile([P, S], U8, name="v_plane", align_bytes=64)
+        w1_q = {}
+        nc.vector.tensor_copy(v_words[0][:], tab_sb[0][:].indirect(offs_sb[:]))
+        nc.vector.tensor_copy(v_plane[:], tab_plane[:].indirect(offs_sb[:]))
+        w1_q[0, 0] = quantise(weave_w1("scalar", w1_raw[0, 0]), BANK, "w1_00")
+        nc.vector.tensor_copy(v_words[1][:], tab_sb[1][:].indirect(offs_sb[:]))
+        woven_last = woven_tile(BANK)
+        for half, engine in enumerate(("scalar", "vector")):
+            copy_on(
+                engine,
+                woven_last[:].rearrange("p (t m j) -> p m j t", t=PACK, j=PACK)[:, half * 64 : (half + 1) * 64],
+                w1_last[half][:].rearrange("p j (m t) -> p m j t", t=PACK),
+            )
+        w1_q[1, 0] = quantise(woven_last, BANK, "w1_10", pieces=PACK)
+
+        bounded, h = {}, {}
+
+        def first_product(i):
+            b, t = divmod(i, PACK)
+            bounded[i] = ring.tile([P, S], F32, name="bounded", tag="bounded", bufs=3)
+            for half in range(S // BANK):
+                cols = slice(half * BANK, (half + 1) * BANK)
+                e = bank((2 * i + half) % BANKS, "e")
+                for a in range(PASSES):
+                    codes, plane = w1_q[a, b]
+                    nc.tensor.matmul_mx(
+                        out=e[:],
+                        lhsT=codes[:, t * P : (t + 1) * P].bitcast(FP8X4),
+                        lhsT_scale=plane[:, t * P : (t + 1) * P],
+                        rhs=v_words[a][:, cols].bitcast(FP8X4),
+                        rhs_scale=v_plane[4 * a : P, cols],
+                        start=(a == 0),
+                        stop=(a == PASSES - 1),
+                    )
+                nc.scalar.activation(bounded[i][:, cols], e[:], ACT.Tanh)
+
+        def make_h(i):
+            b, t = divmod(i, PACK)
+            h[i] = ring.tile([P, S], F32, name="h", tag="h", bufs=5)
+            step = BANK if i == 0 else S
+            for c in range(0, S, step):
+                cols = slice(c, c + step)
+                nc.vector.scalar_tensor_tensor(
+                    h[i][:, cols], bounded[i][:, cols], gain_sb[:, b, t : t + 1], visit_sb[i][:, cols], ALU.mult, ALU.add
+                )
+
+        def pick(i, places, first, count):
+            picked = ring.tile([P, PICKS], F32, name="picked", tag="picked", bufs=4)
+            nc.vector.tensor_copy(
+                picked[:, 0:count], h[i][:].indirect(places[:, first // LIST : (first + count) // LIST])
+            )
+            return picked[:, 0:count]
+
+        def weigh_pain(i, rows, picked):
+            b, t = divmod(i, PACK)
+            nc.scalar.activation(rows[:, t, :], picked, ACT.Copy, scale=pain_sb[:, b, t : t + 1])
+
+        def floor_breath(i, rows, picked):
+            b, t = divmod(i, PACK)
+            nc.vector.tensor_scalar(rows[:, t, :], picked, breath_sb[:, b, t : t + 1], None, ALU.max)
+
+        xa_rows = [keep.tile([P, PACK, PICKS], BF16, name="xa_rows%d" % b) for b in range(PASSES)]
+        xb_rows0 = keep.tile([P, PACK, PICKS], BF16, name="xb_rows0")
+        xb_rows1 = [keep.tile([P, PACK, HALF], BF16, name="xb_rows1_%d" % m) for m in range(2)]
+        xa_q, wb_q = {}, {}
+
+        first_product(0)
+        first_product(1)
+        make_h(0)
+        for i in range(PACK):
+            make_h(i + 1)
+            first_product(i + 2)
+            for_b = pick(i, pos2_sb, 0, PICKS)
+            for_a = pick(i, pos1_sb, 0, PICKS)
+            floor_breath(i, xb_rows0, for_b)
+            weigh_pain(i, xa_rows[0], for_a)
+            if i < PASSES:
+                w1_q[i, 1] = quantise(weave_w1("scalar", w1_raw[i, 1]), BANK, "w1_%d1" % i)
+            else:
+                b = i - PASSES
+                wb_q[b] = quantise(weave("scalar", wb_raw[b], N), N, "wb%d" % b)
+        for i in range(PACK, ROW_TILES):
+            if i + 1 < ROW_TILES:
+                make_h(i + 1)
+            if i + 2 < ROW_TILES:
+                first_product(i + 2)
+            weigh_pain(i, xa_rows[1], pick(i, pos1_sb, 0, PICKS))
+            if i == PACK:
+                xa_q[0] = quantise(weave("scalar", xa_rows[0], PICKS), PICKS, "xa0")
+            if i == PACK + 1:
+                xb_q0 = quantise(weave("scalar", xb_rows0, PICKS), PICKS, "xb0")
+
+        ya = [bank(n, "ya") for n in range(4)]
+        yb = {(m, pair): bank(4 + 2 * m + pair, "yb") for m in range(2) for pair in range(2)}
+
+        def ya_pass(b):
+            codes, plane = xa_q[b]
+            for n in range(4):
+                nc.tensor.matmul_mx(
+                    out=ya[n][:],
+                    lhsT=wa_sb[:, b, 2 * n * P : 2 * (n + 1) * P].bitcast(FP4X4),
+                    lhsT_scale=wa_plane[:, b, n * P : (n + 1) * P],
+                    rhs=codes[:].bitcast(FP8X4),
+                    rhs_scale=plane[:],
+                    start=(b == 0),
+                    stop=(b == PASSES - 1),
+                )
+
+        def yb_pass(b, m, codes, plane):
+            w_codes, w_plane = wb_q[b]
+            for n in range(4):
+                pair, side = divmod(n, 2)
+                nc.tensor.matmul_mx(
+                    out=yb[m, pair][:, side * HALF : (side + 1) * HALF],
+                    lhsT=w_codes[:, n * P : (n + 1) * P].bitcast(FP8X4),
+                    lhsT_scale=w_plane[:, n * P : (n + 1) * P],
+                    rhs=codes.bitcast(FP8X4),
+                    rhs_scale=plane,
+                    start=(b == 0 and side == 0),
+                    stop=(b == PASSES - 1 and side == 1),
+                )
+
+        ya_pass(0)
+        for m in range(2):
+            cols = slice(m * HALF, (m + 1) * HALF)
+            yb_pass(0, m, xb_q0[0][:, cols], xb_q0[1][:, cols])
+
+        def pick_breath_half(m, picked):
+            places = pos2_sb[:, m * HALF // LIST : (m + 1) * HALF // LIST]
+            for t in range(PACK + 1):
+                if t < PACK:
+                    nc.vector.tensor_copy(picked[:, t, :], h[PACK + t][:].indirect(places))
+                if t > 0:
+                    floor_breath(PACK + t - 1, xb_rows1[m], picked[:, t - 1, :])
+
+        ya_sb = [keep.tile([P, 2, PICKS], F32, name="ya_sb%d" % pair) for pair in range(2)]
+        xa_woven = weave("scalar", xa_rows[1], PICKS, tag="late_a", bufs=1)
+        picked0 = keep.tile([P, PACK, HALF], F32, name="picked0")
+        pick_breath_half(0, picked0)
+        xa_q[1] = quantise(xa_woven, PICKS, "xa1")
+        ya_pass(1)
+        xb_woven0 = weave("scalar", xb_rows1[0], HALF)
+        for n in range(4):
+            nc.scalar.copy(ya_sb[n // 2][:, n % 2, :], ya[n][:])
+        picked1 = ring.tile([P, PACK, HALF], F32, name="picked1", tag="late_a", bufs=1, align_bytes=64)
+        pick_breath_half(1, picked1)
+        codes, plane = quantise(xb_woven0, HALF, "xb1_0")
+        yb_pass(1, 0, codes[:], plane[:])
+        xb_woven1 = weave("scalar", xb_rows1[1], HALF, tag="late_b", bufs=1)
+
+        out_view = out.rearrange("(n p) m -> p n m", p=P)
+
+        def finish(m, pair, tag="larger", bufs=2):
+            cols = slice(m * HALF, (m + 1) * HALF)
+            ya_part = ya_sb[pair][:, :, cols]
+            larger = ring.tile([P, 2, HALF], F32, name="larger", tag=tag, bufs=bufs, align_bytes=64)
+            nc.vector.tensor_tensor(larger[:], yb[m, pair][:].rearrange("p (n m) -> p n m", n=2), ya_part, ALU.max)
+            result = ring.tile([P, 2, HALF], F32, name="result", tag="result", bufs=4)
+            nc.vector.tensor_tensor(result[:], larger[:], ya_part, ALU.add)
+            nc.sync.dma_start(out_view[:, 2 * pair : 2 * pair + 2, cols], result[:])
+
+        finish(0, 0)
+        codes, plane = quantise(xb_woven1, HALF, "xb1_1")
+        yb_pass(1, 1, codes[:], plane[:])
+        finish(0, 1, tag="late_b", bufs=1)
+        finish(1, 0)
+        finish(1, 1)

@@ -46,16 +46,13 @@ def tile_list_symptom_diary_features_kernel(
             return tile
 
         def load_rows(src, name):
-            raw = ring.tile([P, PACK, BANK], F32, name=name, tag="raw", bufs=3)
+            raw = ring.tile([P, PACK, BANK], F32, name=name, tag="raw", bufs=4)
             nc.sync.dma_start(raw[:], src.rearrange("(p j) c -> p j c", j=PACK))
             return raw
 
-        def load_table(a, pieces):
-            words = keep.tile([P, T], U32, name="tab_words%d" % a)
-            src = tab_words[a].rearrange("p t i -> p (t i)").bitcast(I32)
-            step = T // pieces
-            for c in range(0, T, step):
-                nc.sync.dma_start(words[:, c : c + step].bitcast(I32), src[:, c : c + step])
+        def load_table(a):
+            words = keep.tile([P, T], U32, name="tab_words", tag="table%d" % a, align_bytes=64)
+            nc.sync.dma_start(words[:].bitcast(I32), tab_words[a].rearrange("p t i -> p (t i)").bitcast(I32))
             return words
 
         def load_vector(src, name):
@@ -65,29 +62,30 @@ def tile_list_symptom_diary_features_kernel(
 
         def load_visit(i):
             b, t = divmod(i, PACK)
-            tile = keep.tile([P, S], F32, name="visit%d" % i)
+            if i == 0:
+                tile = ring.tile([P, S], F32, name="visit", tag="visit0", bufs=1, align_bytes=64)
+            else:
+                tile = ring.tile([P, S], F32, name="visit", tag="visit", bufs=5)
             nc.sync.dma_start(tile[:], visit.rearrange("(b p t) j -> b t p j", b=PASSES, t=PACK)[b, t])
             return tile
 
         def w1_block(a, b):
             return w1[a * K_PASS : (a + 1) * K_PASS, b * K_PASS : (b + 1) * K_PASS]
 
-        tab_plane = keep.tile([P, T], U8, name="tab_plane")
+        tab_plane = keep.tile([P, T], U8, name="tab_plane", tag="tab_plane", align_bytes=64)
         nc.vector.memset(tab_plane[:].bitcast(I32), 0)
         wa_plane = keep.tile([P, PASSES, N], U8, name="wa_plane", align_bytes=64)
         nc.vector.memset(wa_plane[:].rearrange("p a c -> p (a c)").bitcast(I32), 0)
+
         tab_sb, w1_raw, wb_raw, visit_sb = {}, {}, {}, {}
         offs_sb = load_list(offs, "offs_sb")
-        pos2_sb = load_list(pos2, "pos2_sb")
-        pos1_sb = load_list(pos1, "pos1_sb")
-        gain_sb = load_vector(gain, "gain_sb")
-        tab_sb[0] = load_table(0, 4)
+        tab_sb[0] = load_table(0)
         for q in range(4):
-            nc.scalar.dma_start(
+            nc.gpsimd.dma_start(
                 tab_plane[32 * q : 32 * q + 4 * PASSES, :].bitcast(I32), tab_scales[:, 4 * q : 4 * q + 4, :].bitcast(I32)
             )
         w1_raw[0, 0] = load_rows(w1_block(0, 0), "w1_raw")
-        tab_sb[1] = load_table(1, 1)
+        tab_sb[1] = load_table(1)
         w1_last = []
         for half in range(2):
             raw = keep.tile([P, PACK, HALF], F32, name="w1_last%d" % half)
@@ -95,12 +93,16 @@ def tile_list_symptom_diary_features_kernel(
                 raw[:], w1_block(1, 0)[:, half * HALF : (half + 1) * HALF].rearrange("(p j) c -> p j c", j=PACK)
             )
             w1_last.append(raw)
+        gain_sb = load_vector(gain, "gain_sb")
         visit_sb[0] = load_visit(0)
+        visit_sb[1] = load_visit(1)
+        pos2_sb = load_list(pos2, "pos2_sb")
+        pos1_sb = load_list(pos1, "pos1_sb")
         breath_sb = load_vector(breath, "breath_sb")
         pain_sb = load_vector(pain, "pain_sb")
         for a in range(PASSES):
-            visit_sb[1 + a] = load_visit(1 + a)
             w1_raw[a, 1] = load_rows(w1_block(a, 1), "w1_raw")
+        visit_sb[2] = load_visit(2)
         for b in range(PASSES):
             visit_sb[3 + b] = load_visit(3 + b)
             wb_raw[b] = load_rows(wb[b * K_PASS : (b + 1) * K_PASS, :], "wb_raw")
@@ -132,8 +134,16 @@ def tile_list_symptom_diary_features_kernel(
             )
             return woven
 
-        def weave_w1(engine, raw):
-            woven = woven_tile(BANK)
+        def weave_pairs(pairs, width, tag="woven", bufs=3):
+            woven = woven_tile(width, tag, bufs)
+            nc.scalar.copy(
+                woven[:].bitcast(U32).rearrange("p (c u) -> p c u", u=2),
+                pairs[:].bitcast(U32).rearrange("p u c -> p c u"),
+            )
+            return woven
+
+        def weave_w1(engine, raw, tag="woven", bufs=3):
+            woven = woven_tile(BANK, tag, bufs)
             copy_on(
                 engine,
                 woven[:].rearrange("p (t m j) -> p m j t", t=PACK, j=PACK),
@@ -141,8 +151,8 @@ def tile_list_symptom_diary_features_kernel(
             )
             return woven
 
-        def quantise(woven, width, name, pieces=1):
-            codes = keep.tile([P, width], U32, name=name + "_codes", align_bytes=64)
+        def quantise(woven, width, name, pieces=1, tag=""):
+            codes = keep.tile([P, width], U32, name=name + "_codes", tag=tag, align_bytes=64)
             plane = keep.tile([P, width], U8, name=name + "_plane", align_bytes=64)
             step = width // pieces
             for c in range(0, width, step):
@@ -153,14 +163,15 @@ def tile_list_symptom_diary_features_kernel(
                 )
             return codes, plane
 
-        v_words = [keep.tile([P, S], U32, name="v_words%d" % a, align_bytes=64) for a in range(PASSES)]
-        v_plane = keep.tile([P, S], U8, name="v_plane", align_bytes=64)
-        w1_q = {}
+        w1_q, v_words = {}, {}
+        v_words[0] = keep.tile([P, S], U32, name="v_words0", align_bytes=64)
         nc.vector.tensor_copy(v_words[0][:], tab_sb[0][:].indirect(offs_sb[:]))
+        v_plane = keep.tile([P, S], U8, name="v_plane", tag="table0", align_bytes=64)
         nc.vector.tensor_copy(v_plane[:], tab_plane[:].indirect(offs_sb[:]))
-        w1_q[0, 0] = quantise(weave_w1("scalar", w1_raw[0, 0]), BANK, "w1_00")
+        w1_q[0, 0] = quantise(weave_w1("scalar", w1_raw[0, 0], "first", 1), BANK, "w1_00", tag="tab_plane")
+        v_words[1] = ring.tile([P, S], U32, name="v_words1", tag="first", bufs=1, align_bytes=64)
         nc.vector.tensor_copy(v_words[1][:], tab_sb[1][:].indirect(offs_sb[:]))
-        woven_last = woven_tile(BANK)
+        woven_last = keep.tile([P, PACK * BANK], BF16, name="woven_last", tag="table1", align_bytes=64)
         for half, engine in enumerate(("scalar", "vector")):
             copy_on(
                 engine,
@@ -171,10 +182,13 @@ def tile_list_symptom_diary_features_kernel(
 
         bounded, h = {}, {}
 
+        def slot_tile(i, half, name):
+            return ring.tile([P, BANK], F32, name=name, tag="slot%d_%d" % (i % 4, half), bufs=1)
+
         def first_product(i):
             b, t = divmod(i, PACK)
-            bounded[i] = ring.tile([P, S], F32, name="bounded", tag="bounded", bufs=3)
             for half in range(S // BANK):
+                bounded[i, half] = slot_tile(i, half, "bounded")
                 cols = slice(half * BANK, (half + 1) * BANK)
                 e = bank((2 * i + half) % BANKS, "e")
                 for a in range(PASSES):
@@ -188,34 +202,37 @@ def tile_list_symptom_diary_features_kernel(
                         start=(a == 0),
                         stop=(a == PASSES - 1),
                     )
-                nc.scalar.activation(bounded[i][:, cols], e[:], ACT.Tanh)
+                nc.scalar.activation(bounded[i, half][:], e[:], ACT.Tanh)
 
         def make_h(i):
             b, t = divmod(i, PACK)
             h[i] = ring.tile([P, S], F32, name="h", tag="h", bufs=5)
-            step = BANK if i == 0 else S
-            for c in range(0, S, step):
-                cols = slice(c, c + step)
+            for half in range(S // BANK):
+                cols = slice(half * BANK, (half + 1) * BANK)
                 nc.vector.scalar_tensor_tensor(
-                    h[i][:, cols], bounded[i][:, cols], gain_sb[:, b, t : t + 1], visit_sb[i][:, cols], ALU.mult, ALU.add
+                    h[i][:, cols], bounded[i, half][:], gain_sb[:, b, t : t + 1], visit_sb[i][:, cols], ALU.mult, ALU.add
                 )
 
-        def pick(i, places, first, count):
-            picked = ring.tile([P, PICKS], F32, name="picked", tag="picked", bufs=4)
-            nc.vector.tensor_copy(
-                picked[:, 0:count], h[i][:].indirect(places[:, first // LIST : (first + count) // LIST])
-            )
-            return picked[:, 0:count]
+        def pick(i, places, half):
+            if (i, half) == (2, 0):
+                picked = ring.tile([P, PICKS], F32, name="picked", tag="late_a", bufs=1, align_bytes=64)
+            else:
+                picked = slot_tile(i + 1, half, "picked")
+            nc.vector.tensor_copy(picked[:], h[i][:].indirect(places[:]))
+            return picked[:]
+
+        def pair_slot(pairs, t):
+            return pairs[:, t // 2, :].rearrange("p (c e) -> p c e", e=2)[:, :, t % 2]
 
         def weigh_pain(i, rows, picked):
             b, t = divmod(i, PACK)
-            nc.scalar.activation(rows[:, t, :], picked, ACT.Copy, scale=pain_sb[:, b, t : t + 1])
+            nc.scalar.activation(pair_slot(rows, t), picked, ACT.Copy, scale=pain_sb[:, b, t : t + 1])
 
         def floor_breath(i, rows, picked):
             b, t = divmod(i, PACK)
             nc.vector.tensor_scalar(rows[:, t, :], picked, breath_sb[:, b, t : t + 1], None, ALU.max)
 
-        xa_rows = [keep.tile([P, PACK, PICKS], BF16, name="xa_rows%d" % b) for b in range(PASSES)]
+        xa_rows = [keep.tile([P, 2, 2 * PICKS], BF16, name="xa_rows%d" % b) for b in range(PASSES)]
         xb_rows0 = keep.tile([P, PACK, PICKS], BF16, name="xb_rows0")
         xb_rows1 = [keep.tile([P, PACK, HALF], BF16, name="xb_rows1_%d" % m) for m in range(2)]
         xa_q, wb_q = {}, {}
@@ -226,13 +243,15 @@ def tile_list_symptom_diary_features_kernel(
         for i in range(PACK):
             make_h(i + 1)
             first_product(i + 2)
-            for_b = pick(i, pos2_sb, 0, PICKS)
-            for_a = pick(i, pos1_sb, 0, PICKS)
+            if i == 0:
+                w1_q[0, 1] = quantise(weave_w1("scalar", w1_raw[0, 1], "visit0", 1), BANK, "w1_01")
+            if i == 1:
+                w1_q[1, 1] = quantise(weave_w1("scalar", w1_raw[1, 1], "late_a", 1), BANK, "w1_11")
+            for_b = pick(i, pos2_sb, 0)
+            for_a = pick(i, pos1_sb, 1)
             floor_breath(i, xb_rows0, for_b)
             weigh_pain(i, xa_rows[0], for_a)
-            if i < PASSES:
-                w1_q[i, 1] = quantise(weave_w1("scalar", w1_raw[i, 1]), BANK, "w1_%d1" % i)
-            else:
+            if i >= PASSES:
                 b = i - PASSES
                 wb_q[b] = quantise(weave("scalar", wb_raw[b], N), N, "wb%d" % b)
         for i in range(PACK, ROW_TILES):
@@ -240,9 +259,9 @@ def tile_list_symptom_diary_features_kernel(
                 make_h(i + 1)
             if i + 2 < ROW_TILES:
                 first_product(i + 2)
-            weigh_pain(i, xa_rows[1], pick(i, pos1_sb, 0, PICKS))
+            weigh_pain(i, xa_rows[1], pick(i, pos1_sb, 0))
             if i == PACK:
-                xa_q[0] = quantise(weave("scalar", xa_rows[0], PICKS), PICKS, "xa0")
+                xa_q[0] = quantise(weave_pairs(xa_rows[0], PICKS), PICKS, "xa0")
             if i == PACK + 1:
                 xb_q0 = quantise(weave("scalar", xb_rows0, PICKS), PICKS, "xb0")
 
@@ -290,7 +309,7 @@ def tile_list_symptom_diary_features_kernel(
                     floor_breath(PACK + t - 1, xb_rows1[m], picked[:, t - 1, :])
 
         ya_sb = [keep.tile([P, 2, PICKS], F32, name="ya_sb%d" % pair) for pair in range(2)]
-        xa_woven = weave("scalar", xa_rows[1], PICKS, tag="late_a", bufs=1)
+        xa_woven = weave_pairs(xa_rows[1], PICKS, tag="late_a", bufs=1)
         picked0 = keep.tile([P, PACK, HALF], F32, name="picked0")
         pick_breath_half(0, picked0)
         xa_q[1] = quantise(xa_woven, PICKS, "xa1")
@@ -306,18 +325,23 @@ def tile_list_symptom_diary_features_kernel(
 
         out_view = out.rearrange("(n p) m -> p n m", p=P)
 
-        def finish(m, pair, tag="larger", bufs=2):
-            cols = slice(m * HALF, (m + 1) * HALF)
-            ya_part = ya_sb[pair][:, :, cols]
-            larger = ring.tile([P, 2, HALF], F32, name="larger", tag=tag, bufs=bufs, align_bytes=64)
+        def take_larger(m, pair):
+            larger = ring.tile([P, 2, HALF], F32, name="larger", tag="larger", bufs=2)
+            ya_part = ya_sb[pair][:, :, m * HALF : (m + 1) * HALF]
             nc.vector.tensor_tensor(larger[:], yb[m, pair][:].rearrange("p (n m) -> p n m", n=2), ya_part, ALU.max)
-            result = ring.tile([P, 2, HALF], F32, name="result", tag="result", bufs=4)
-            nc.vector.tensor_tensor(result[:], larger[:], ya_part, ALU.add)
+            return larger
+
+        def finish(m, pair, larger, tag="result", bufs=3):
+            cols = slice(m * HALF, (m + 1) * HALF)
+            result = ring.tile([P, 2, HALF], F32, name="result", tag=tag, bufs=bufs, align_bytes=64)
+            nc.vector.tensor_tensor(result[:], larger[:], ya_sb[pair][:, :, cols], ALU.add)
             nc.sync.dma_start(out_view[:, 2 * pair : 2 * pair + 2, cols], result[:])
 
-        finish(0, 0)
+        larger = [take_larger(0, pair) for pair in range(2)]
         codes, plane = quantise(xb_woven1, HALF, "xb1_1")
         yb_pass(1, 1, codes[:], plane[:])
-        finish(0, 1, tag="late_b", bufs=1)
-        finish(1, 0)
-        finish(1, 1)
+        finish(0, 0, larger[0], tag="late_b", bufs=1)
+        finish(0, 1, larger[1])
+        larger = [take_larger(1, pair) for pair in range(2)]
+        for pair in range(2):
+            finish(1, pair, larger[pair])

from contextlib import ExitStack

import concourse.mybir as mybir

K, H, N, T, S, PICKS = 1024, 1024, 512, 4096, 1024, 512
FLOPS = 2 * K * H * S + 2 * 2 * H * N * PICKS

F32 = mybir.dt.float32
BF16 = mybir.dt.bfloat16
I32 = mybir.dt.int32
U32 = mybir.dt.uint32
U16 = mybir.dt.uint16
U8 = mybir.dt.uint8
FP8X4 = mybir.dt.float8_e4m3fn_x4
FP4X4 = mybir.dt.float4_e2m1fn_x4
ALU = mybir.AluOpType
ACT = mybir.ActivationFunctionType

P = 128
PACK = 4
K_PASS = P * PACK
PASSES = 2
BANK = 512
BANKS = 8
LIST = 16
HALF = PICKS // 2
ROW_TILES = PASSES * PACK


def tile_list_symptom_diary_features_kernel(
    tc, tab_words, tab_scales, offs, pos1, pos2, w1, gain, visit, pain, breath, wa_words, wa_scales, wb, out
):
    nc = tc.nc
    with ExitStack() as ctx:
        lists = ctx.enter_context(tc.tile_pool(name="lists", bufs=1))
        keep = ctx.enter_context(tc.tile_pool(name="keep", bufs=1))
        ring = ctx.enter_context(tc.tile_pool(name="ring", bufs=2))
        psum = ctx.enter_context(tc.psum_pool(name="psum", bufs=1))

        def bank(k, name):
            return psum.tile([P, BANK], F32, name=name, tag="bank%d" % k)

        def load_list(src, name):
            tile = lists.tile([P, src.shape[1]], U16, name=name)
            nc.sync.dma_start(tile[:], src)
            return tile

        def load_rows(src, name):
            raw = ring.tile([P, PACK, BANK], F32, name=name, tag="raw", bufs=4)
            nc.sync.dma_start(raw[:], src.rearrange("(p j) c -> p j c", j=PACK))
            return raw

        def load_table(a):
            words = keep.tile([P, T], U32, name="tab_words", tag="table%d" % a, align_bytes=64)
            nc.sync.dma_start(words[:].bitcast(I32), tab_words[a].rearrange("p t i -> p (t i)").bitcast(I32))
            return words

        def load_vector(src, name):
            tile = keep.tile([P, PASSES, 2 * PACK], F32, name=name)
            nc.sync.dma_start(tile[:, :, 0:PACK], src.rearrange("(b p t) -> p b t", b=PASSES, t=PACK))
            return tile

        def load_visit(i):
            b, t = divmod(i, PACK)
            if i == 0:
                tile = ring.tile([P, S], F32, name="visit", tag="visit0", bufs=1, align_bytes=64)
            else:
                tile = ring.tile([P, S], F32, name="visit", tag="visit", bufs=5)
            nc.sync.dma_start(tile[:], visit.rearrange("(b p t) j -> b t p j", b=PASSES, t=PACK)[b, t])
            return tile

        def w1_block(a, b):
            return w1[a * K_PASS : (a + 1) * K_PASS, b * K_PASS : (b + 1) * K_PASS]

        tab_plane = keep.tile([P, T], U8, name="tab_plane", tag="tab_plane", align_bytes=64)
        nc.vector.memset(tab_plane[:].bitcast(I32), 0)
        wa_plane = keep.tile([P, PASSES, N], U8, name="wa_plane", align_bytes=64)
        nc.vector.memset(wa_plane[:].rearrange("p a c -> p (a c)").bitcast(I32), 0)

        tab_sb, w1_raw, wb_raw, visit_sb = {}, {}, {}, {}
        offs_sb = load_list(offs, "offs_sb")
        tab_sb[0] = load_table(0)
        for q in range(4):
            nc.gpsimd.dma_start(
                tab_plane[32 * q : 32 * q + 4 * PASSES, :].bitcast(I32), tab_scales[:, 4 * q : 4 * q + 4, :].bitcast(I32)
            )
        w1_raw[0, 0] = load_rows(w1_block(0, 0), "w1_raw")
        tab_sb[1] = load_table(1)
        w1_last = []
        for half in range(2):
            raw = keep.tile([P, PACK, HALF], F32, name="w1_last%d" % half)
            nc.sync.dma_start(
                raw[:], w1_block(1, 0)[:, half * HALF : (half + 1) * HALF].rearrange("(p j) c -> p j c", j=PACK)
            )
            w1_last.append(raw)
        gain_sb = load_vector(gain, "gain_sb")
        visit_sb[0] = load_visit(0)
        visit_sb[1] = load_visit(1)
        pos2_sb = load_list(pos2, "pos2_sb")
        pos1_sb = load_list(pos1, "pos1_sb")
        breath_sb = load_vector(breath, "breath_sb")
        pain_sb = load_vector(pain, "pain_sb")
        for a in range(PASSES):
            w1_raw[a, 1] = load_rows(w1_block(a, 1), "w1_raw")
        visit_sb[2] = load_visit(2)
        for b in range(PASSES):
            visit_sb[3 + b] = load_visit(3 + b)
            wb_raw[b] = load_rows(wb[b * K_PASS : (b + 1) * K_PASS, :], "wb_raw")
        for i in range(5, ROW_TILES):
            visit_sb[i] = load_visit(i)
        wa_sb = keep.tile([P, PASSES, 2 * N], U8, name="wa_sb", align_bytes=64)
        nc.sync.dma_start(wa_sb[:].bitcast(I32), wa_words.rearrange("a p c -> p a c").bitcast(I32))
        for q in range(4):
            nc.sync.dma_start(
                wa_plane[32 * q : 32 * q + 4].bitcast(I32),
                wa_scales[:, 4 * q : 4 * q + 4, :].rearrange("a r c -> r a c").bitcast(I32),
            )

        def copy_on(engine, dst, src):
            if engine == "scalar":
                nc.scalar.copy(dst, src)
            else:
                nc.vector.tensor_copy(dst, src)

        def woven_tile(width, tag="woven", bufs=3):
            return ring.tile([P, PACK * width], BF16, name="woven", tag=tag, bufs=bufs, align_bytes=64)

        def weave(engine, rows, width, tag="woven", bufs=3):
            woven = woven_tile(width, tag, bufs)
            copy_on(
                engine,
                woven[:].rearrange("p (c i j) -> p c j i", i=4, j=PACK),
                rows[:].rearrange("p j (c i) -> p c j i", i=4),
            )
            return woven

        def weave_pairs(pairs, width, tag="woven", bufs=3):
            woven = woven_tile(width, tag, bufs)
            nc.scalar.copy(
                woven[:].bitcast(U32).rearrange("p (c u) -> p c u", u=2),
                pairs[:].bitcast(U32).rearrange("p u c -> p c u"),
            )
            return woven

        def weave_w1(engine, raw, tag="woven", bufs=3):
            woven = woven_tile(BANK, tag, bufs)
            copy_on(
                engine,
                woven[:].rearrange("p (t m j) -> p m j t", t=PACK, j=PACK),
                raw[:].rearrange("p j (m t) -> p m j t", t=PACK),
            )
            return woven

        def quantise(woven, width, name, pieces=1, tag=""):
            codes = keep.tile([P, width], U32, name=name + "_codes", tag=tag, align_bytes=64)
            plane = keep.tile([P, width], U8, name=name + "_plane", align_bytes=64)
            step = width // pieces
            for c in range(0, width, step):
                nc.vector.quantize_mx(
                    out=codes[:, c : c + step].bitcast(FP8X4),
                    scales=plane[:, c : c + step],
                    in_=woven[:, PACK * c : PACK * (c + step)],
                )
            return codes, plane

        w1_q, v_words = {}, {}
        v_words[0] = keep.tile([P, S], U32, name="v_words0", align_bytes=64)
        nc.vector.tensor_copy(v_words[0][:], tab_sb[0][:].indirect(offs_sb[:]))
        v_plane = keep.tile([P, S], U8, name="v_plane", tag="table0", align_bytes=64)
        nc.vector.tensor_copy(v_plane[:], tab_plane[:].indirect(offs_sb[:]))
        w1_q[0, 0] = quantise(weave_w1("scalar", w1_raw[0, 0], "first", 1), BANK, "w1_00", tag="tab_plane")
        v_words[1] = ring.tile([P, S], U32, name="v_words1", tag="first", bufs=1, align_bytes=64)
        nc.vector.tensor_copy(v_words[1][:], tab_sb[1][:].indirect(offs_sb[:]))
        woven_last = keep.tile([P, PACK * BANK], BF16, name="woven_last", tag="table1", align_bytes=64)
        for half, engine in enumerate(("scalar", "vector")):
            copy_on(
                engine,
                woven_last[:].rearrange("p (t m j) -> p m j t", t=PACK, j=PACK)[:, half * 64 : (half + 1) * 64],
                w1_last[half][:].rearrange("p j (m t) -> p m j t", t=PACK),
            )
        w1_q[1, 0] = quantise(woven_last, BANK, "w1_10", pieces=PACK)

        bounded, h = {}, {}

        def slot_tile(i, half, name):
            return ring.tile([P, BANK], F32, name=name, tag="slot%d_%d" % (i % 4, half), bufs=1)

        def first_product(i):
            b, t = divmod(i, PACK)
            for half in range(S // BANK):
                bounded[i, half] = slot_tile(i, half, "bounded")
                cols = slice(half * BANK, (half + 1) * BANK)
                e = bank((2 * i + half) % BANKS, "e")
                for a in range(PASSES):
                    codes, plane = w1_q[a, b]
                    nc.tensor.matmul_mx(
                        out=e[:],
                        lhsT=codes[:, t * P : (t + 1) * P].bitcast(FP8X4),
                        lhsT_scale=plane[:, t * P : (t + 1) * P],
                        rhs=v_words[a][:, cols].bitcast(FP8X4),
                        rhs_scale=v_plane[4 * a : P, cols],
                        start=(a == 0),
                        stop=(a == PASSES - 1),
                    )
                nc.scalar.activation(bounded[i, half][:], e[:], ACT.Tanh)

        def make_h(i):
            b, t = divmod(i, PACK)
            h[i] = ring.tile([P, S], F32, name="h", tag="h", bufs=5)
            for half in range(S // BANK):
                cols = slice(half * BANK, (half + 1) * BANK)
                nc.vector.scalar_tensor_tensor(
                    h[i][:, cols], bounded[i, half][:], gain_sb[:, b, t : t + 1], visit_sb[i][:, cols], ALU.mult, ALU.add
                )

        def pick(i, places, half):
            if (i, half) == (2, 0):
                picked = ring.tile([P, PICKS], F32, name="picked", tag="late_a", bufs=1, align_bytes=64)
            else:
                picked = slot_tile(i + 1, half, "picked")
            nc.vector.tensor_copy(picked[:], h[i][:].indirect(places[:]))
            return picked[:]

        def pair_slot(pairs, t):
            return pairs[:, t // 2, :].rearrange("p (c e) -> p c e", e=2)[:, :, t % 2]

        def weigh_pain(i, rows, picked):
            b, t = divmod(i, PACK)
            nc.scalar.activation(pair_slot(rows, t), picked, ACT.Copy, scale=pain_sb[:, b, t : t + 1])

        def floor_breath(i, rows, picked):
            b, t = divmod(i, PACK)
            nc.vector.tensor_scalar(rows[:, t, :], picked, breath_sb[:, b, t : t + 1], None, ALU.max)

        xa_rows = [keep.tile([P, 2, 2 * PICKS], BF16, name="xa_rows%d" % b) for b in range(PASSES)]
        xb_rows0 = keep.tile([P, PACK, PICKS], BF16, name="xb_rows0")
        xb_rows1 = [keep.tile([P, PACK, HALF], BF16, name="xb_rows1_%d" % m) for m in range(2)]
        xa_q, wb_q = {}, {}

        first_product(0)
        first_product(1)
        make_h(0)
        for i in range(PACK):
            make_h(i + 1)
            first_product(i + 2)
            if i == 0:
                w1_q[0, 1] = quantise(weave_w1("scalar", w1_raw[0, 1], "visit0", 1), BANK, "w1_01")
            if i == 1:
                w1_q[1, 1] = quantise(weave_w1("scalar", w1_raw[1, 1], "late_a", 1), BANK, "w1_11")
            for_b = pick(i, pos2_sb, 0)
            for_a = pick(i, pos1_sb, 1)
            floor_breath(i, xb_rows0, for_b)
            weigh_pain(i, xa_rows[0], for_a)
            if i >= PASSES:
                b = i - PASSES
                wb_q[b] = quantise(weave("scalar", wb_raw[b], N), N, "wb%d" % b)
        for i in range(PACK, ROW_TILES):
            if i + 1 < ROW_TILES:
                make_h(i + 1)
            if i + 2 < ROW_TILES:
                first_product(i + 2)
            weigh_pain(i, xa_rows[1], pick(i, pos1_sb, 0))
            if i == PACK:
                xa_q[0] = quantise(weave_pairs(xa_rows[0], PICKS), PICKS, "xa0")
            if i == PACK + 1:
                xb_q0 = quantise(weave("scalar", xb_rows0, PICKS), PICKS, "xb0")

        ya = [bank(n, "ya") for n in range(4)]
        yb = {(m, pair): bank(4 + 2 * m + pair, "yb") for m in range(2) for pair in range(2)}

        def ya_pass(b):
            codes, plane = xa_q[b]
            for n in range(4):
                nc.tensor.matmul_mx(
                    out=ya[n][:],
                    lhsT=wa_sb[:, b, 2 * n * P : 2 * (n + 1) * P].bitcast(FP4X4),
                    lhsT_scale=wa_plane[:, b, n * P : (n + 1) * P],
                    rhs=codes[:].bitcast(FP8X4),
                    rhs_scale=plane[:],
                    start=(b == 0),
                    stop=(b == PASSES - 1),
                )

        def yb_pass(b, m, codes, plane):
            w_codes, w_plane = wb_q[b]
            for n in range(4):
                pair, side = divmod(n, 2)
                nc.tensor.matmul_mx(
                    out=yb[m, pair][:, side * HALF : (side + 1) * HALF],
                    lhsT=w_codes[:, n * P : (n + 1) * P].bitcast(FP8X4),
                    lhsT_scale=w_plane[:, n * P : (n + 1) * P],
                    rhs=codes.bitcast(FP8X4),
                    rhs_scale=plane,
                    start=(b == 0 and side == 0),
                    stop=(b == PASSES - 1 and side == 1),
                )

        ya_pass(0)
        for m in range(2):
            cols = slice(m * HALF, (m + 1) * HALF)
            yb_pass(0, m, xb_q0[0][:, cols], xb_q0[1][:, cols])

        def pick_breath_half(m, picked):
            places = pos2_sb[:, m * HALF // LIST : (m + 1) * HALF // LIST]
            for t in range(PACK + 1):
                if t < PACK:
                    nc.vector.tensor_copy(picked[:, t, :], h[PACK + t][:].indirect(places))
                if t > 0:
                    floor_breath(PACK + t - 1, xb_rows1[m], picked[:, t - 1, :])

        ya_sb = [keep.tile([P, 2, PICKS], F32, name="ya_sb%d" % pair) for pair in range(2)]
        xa_woven = weave_pairs(xa_rows[1], PICKS, tag="late_a", bufs=1)
        picked0 = keep.tile([P, PACK, HALF], F32, name="picked0")
        pick_breath_half(0, picked0)
        xa_q[1] = quantise(xa_woven, PICKS, "xa1")
        ya_pass(1)
        xb_woven0 = weave("scalar", xb_rows1[0], HALF)
        for n in range(4):
            nc.scalar.copy(ya_sb[n // 2][:, n % 2, :], ya[n][:])
        picked1 = ring.tile([P, PACK, HALF], F32, name="picked1", tag="late_a", bufs=1, align_bytes=64)
        pick_breath_half(1, picked1)
        codes, plane = quantise(xb_woven0, HALF, "xb1_0")
        yb_pass(1, 0, codes[:], plane[:])
        xb_woven1 = weave("scalar", xb_rows1[1], HALF, tag="late_b", bufs=1)

        out_view = out.rearrange("(n p) m -> p n m", p=P)

        def take_larger(m, pair):
            larger = ring.tile([P, 2, HALF], F32, name="larger", tag="larger", bufs=2)
            ya_part = ya_sb[pair][:, :, m * HALF : (m + 1) * HALF]
            nc.vector.tensor_tensor(larger[:], yb[m, pair][:].rearrange("p (n m) -> p n m", n=2), ya_part, ALU.max)
            return larger

        def finish(m, pair, larger, tag="result", bufs=3):
            cols = slice(m * HALF, (m + 1) * HALF)
            result = ring.tile([P, 2, HALF], F32, name="result", tag=tag, bufs=bufs, align_bytes=64)
            nc.vector.tensor_tensor(result[:], larger[:], ya_sb[pair][:, :, cols], ALU.add)
            nc.sync.dma_start(out_view[:, 2 * pair : 2 * pair + 2, cols], result[:])

        larger = [take_larger(0, pair) for pair in range(2)]
        codes, plane = quantise(xb_woven1, HALF, "xb1_1")
        yb_pass(1, 1, codes[:], plane[:])
        finish(0, 0, larger[0], tag="late_b", bufs=1)
        finish(0, 1, larger[1])
        larger = [take_larger(1, pair) for pair in range(2)]
        for pair in range(2):
            finish(1, pair, larger[pair])
